import numpy as np, ml_dtypes
CORES = [44,45,46,47,172,173,174,175,300,301,302,303,428,429,430,431]
N = 16
TK = 512
COEF = [[3,1,1,1,1,1,1,1,1,1,1,1,1,1,1,1],[1,3,1,1,1,1,1,1,1,1,1,1,1,1,1,1],[1,1,3,1,1,1,1,1,1,1,1,1,1,1,1,1],[1,1,1,3,1,1,1,1,1,1,1,1,1,1,1,1],[1,1,1,1,3,1,1,1,1,1,1,1,1,1,1,1],[1,1,1,1,1,3,1,1,1,1,1,1,1,1,1,1],[1,1,1,1,1,1,3,1,1,1,1,1,1,1,1,1],[1,1,1,1,1,1,1,3,1,1,1,1,1,1,1,1],[1,1,1,1,1,1,1,1,3,1,1,1,1,1,1,1],[1,1,1,1,1,1,1,1,1,3,1,1,1,1,1,1],[1,1,1,1,1,1,1,1,1,1,3,1,1,1,1,1],[1,1,1,1,1,1,1,1,1,1,1,3,1,1,1,1],[1,1,1,1,1,1,1,1,1,1,1,1,3,1,1,1],[1,1,1,1,1,1,1,1,1,1,1,1,1,3,1,1],[1,1,1,1,1,1,1,1,1,1,1,1,1,1,3,1],[1,1,1,1,1,1,1,1,1,1,1,1,1,1,1,3]]
def setup_inputs(rng):
    return {"x": rng.standard_normal((N, 128, TK), dtype=np.float32).astype(ml_dtypes.bfloat16), "a": (rng.standard_normal((N, 128, 128), dtype=np.float32) / 11).astype(ml_dtypes.bfloat16)}
def setup_inputs_big(rng):
    d = setup_inputs(rng)
    for k in ("x", "a"): d[k] = (d[k].astype(np.float32) * 1024.0).astype(d[k].dtype)
    return d
def setup_inputs_small(rng):
    d = setup_inputs(rng)
    for k in ("x", "a"): d[k] = (d[k].astype(np.float32) * (1 / 1024.0)).astype(d[k].dtype)
    return d
def setup_inputs_apart(rng):
    d = setup_inputs(rng)
    f = (10.0 ** rng.permutation(np.linspace(-1.5, 1.5, N))).astype(np.float32).reshape(N, 1, 1)
    for k in ("x", "a"): d[k] = (d[k].astype(np.float32) * f).astype(d[k].dtype)
    return d
def reference(x, a):
    X, A = x.astype(np.float64), a.astype(np.float64)
    y = np.stack([A[r].T @ sum(COEF[r][j] * X[j] for j in range(N)) for r in range(N)])
    return {"y": y.astype(ml_dtypes.bfloat16)}

@@ -1,0 +1,182 @@
+from concourse.bass import DstId, RemoteDMATransfer
+
+P, TK, NB = 128, 512, 4
+FF = False
+FL = False
+E1, EF, E2, E3, E4 = 2, 2, 8, 8, 8
+
+SCRATCH = {
+    "xd": ("dram", [NB, P, P], "bfloat16"),
+    "L": ("dram", [2 * NB if FF else NB, P, P], "bfloat16"),
+    "su": ("dram", [NB, P, P], "bfloat16"),
+    "sv": ("dram", [NB if FL else 1, P, P], "bfloat16"),
+    "xs": ("sbuf", [P, TK], "bfloat16"),
+    "aw": ("sbuf", [P, P], "bfloat16"),
+    "pb": ("sbuf", [P, (2 * NB if FF else NB) * TK], "bfloat16"),
+    "zu": ("sbuf", [P, TK], "bfloat16"),
+    "zv": ("sbuf", [P, TK if FL else 8], "bfloat16"),
+    "ys": ("sbuf", [P, TK], "bfloat16"),
+    "acc": ("psum", [P, TK], "float32"),
+}
+SEMAPHORES = ["ld", "pre", "pc", "z", "mm", "cp", "st", "l1", "ra", "rb", "ag", "loc1", "loc2", "loc3", "loc4"]
+
+
+def _bits(mask):
+    return [e for e in range(mask.bit_length()) if (mask >> e) & 1]
+
+
+def _mask(engines):
+    m = 0
+    for e in engines:
+        m |= 1 << e
+    return m
+
+
+def rank_program(g, core, T, topo):
+    rank = T.rank_of(core)
+    if rank is None:
+        return
+    S = T.sem
+    coef = T.tables["COEF"]
+    n = len(T.cores)
+    assert all(coef[r][j] == 1 for r in range(n) for j in range(n) if j != r)
+    extra = coef[rank][rank] - 1
+    assert extra >= 0
+
+    def place(c):
+        return (topo.host(c), topo.chip(c))
+
+    chips = []
+    for c in T.cores:
+        if place(c) not in chips:
+            chips.append(place(c))
+    members = {p: [c for c in T.cores if place(c) == p] for p in chips}
+    here = place(core)
+    mine = members[here]
+    assert len(mine) == NB
+    q = mine.index(core)
+    peers = [c for c in mine if c != core]
+    others = [p for p in chips if p != here]
+    sw = [p for p in others if topo.same_plane(core, members[p][q])][0]
+    cb = [p for p in others if topo.rack(p[0]) != topo.rack(here[0]) and topo.may_write(core, members[p][q])][0]
+
+    def near(b):
+        return sw if b % 2 == 0 else cb
+
+    def far(b):
+        return cb if b % 2 == 0 else sw
+
+    off = topo.mask(core, members[sw][q]) & topo.mask(core, members[cb][q])
+    onc = off | 0
+    for c in peers:
+        onc |= topo.mask(core, c)
+    lo = _bits(off)
+    hi = _bits(onc & ~off)
+
+    def to(c):
+        rid, pid = topo.addr(c, core)
+        return DstId(rid=rid, pnc=pid)
+
+    def copy(c, src, dst, engines, sem):
+        return RemoteDMATransfer(dst_ids=[to(c)], dma_engine_mask=_mask(engines), remote_sem=sem, src=src, dst=dst)
+
+    def fold(cs, srcs, dst, engines, sem):
+        return RemoteDMATransfer(dst_ids=[to(c) for c in cs], dma_engine_mask=_mask(engines), remote_sem=sem,
+                                 srcs=srcs, dsts=[dst for c in cs], alu_op=1)
+
+    k0, k1 = q * (P // NB), (q + 1) * (P // NB)
+
+    g.sync.dma_start(T.xd[:], T.x[:]).then_inc(S.ld, 16)
+    g.scalar.wait_ge(S.ld, 16)
+    g.scalar.dma_start(T.xs[:], T.x[:]).then_inc(S.pre, 16)
+    g.scalar.dma_start(T.aw[:], T.a[:]).then_inc(S.pre, 16)
+
+    on1 = hi if FF else lo
+    tr = [copy(c, T.xd[mine.index(c)], T.L[q], on1[E1 * i:E1 * (i + 1)], S.l1) for i, c in enumerate(peers)]
+    n_l1 = E1 * len(peers)
+    if FF:
+        for b in range(NB):
+            dst = T.su[b] if (FL and b == q) else T.L[NB + q]
+            tr.append(copy(members[near(b)][b], T.xd[b], dst, lo[EF * b:EF * (b + 1)], S.l1))
+        n_l1 += EF * NB
+    g.wait_ge(S.ld, 16)
+    g.remote_dma_fused(tr, local_sem=S.loc1)
+    n_loc1 = n_l1
+
+    g.wait_ge(S.l1, n_l1)
+    srcs = [T.xd[q]] + [T.L[b] for b in range(NB) if b != q]
+    pieces = [b for b in range(NB) if b != q]
+    if FF:
+        for s in range(NB):
+            if FL and s == q:
+                srcs.append(T.su[q])
+            else:
+                srcs.append(T.L[NB + s])
+                pieces.append(NB + s)
+    else:
+        spot = T.su[q] if FL else T.L[q]
+        g.remote_dma_fused([fold([members[near(q)][q]], srcs, spot, lo[:E2], S.ra)], local_sem=S.loc2)
+        g.wait_ge(S.ra, E2)
+        srcs = srcs + [spot]
+        if not FL:
+            pieces.append(q)
+
+    if FL:
+        g.remote_dma_fused([fold(members[far(q)], srcs, T.sv[q], lo[:E3], S.rb),
+                            fold(peers, srcs, T.su[q], hi[:E4], S.ag)], local_sem=S.loc3)
+        n_rb, n_loc3 = E3 * NB, E3 + E4
+    else:
+        g.remote_dma_fused([fold([members[far(q)][q]], srcs, T.su[q], lo[:E3], S.rb)], local_sem=S.loc3)
+        n_rb, n_loc3 = E3, E3
+        g.wait_ge(S.rb, n_rb)
+        g.remote_dma_fused([fold(peers, srcs + [T.su[q]], T.su[q], lo[:E4], S.ag)], local_sem=S.loc4)
+    n_ag = E4 * len(peers)
+
+    queues = [g.sync, g.scalar]
+    for Q in queues:
+        Q.wait_ge(S.l1, n_l1)
+        if not FF:
+            Q.wait_ge(S.ra, E2)
+        if not FL:
+            Q.wait_ge(S.loc3, n_loc3)
+        elif not FF:
+            Q.wait_ge(S.loc2, E2)
+    for i, s in enumerate(pieces):
+        queues[i % 2].dma_start(T.pb[k0:k1, i * TK:(i + 1) * TK], T.L[s]).then_inc(S.pc, 16)
+
+    g.sync.wait_ge(S.ag, n_ag)
+    if FL:
+        g.scalar.wait_ge(S.rb, n_rb)
+        g.scalar.dma_start(T.zv[:], T.sv[:]).then_inc(S.z, 16)
+    else:
+        g.sync.wait_ge(S.rb, n_rb)
+    g.sync.dma_start(T.zu[:], T.su[:]).then_inc(S.z, 16)
+
+    mms = [(None, 0, T.aw[:], T.xs[:]) for _ in range(extra)]
+    mms.append((None, 0, T.aw[k0:k1, :], T.xs[k0:k1, :]))
+    mms[0] = (S.pre, 32) + mms[0][2:]
+    for i in range(len(pieces)):
+        mms.append((S.pc if i == 0 else None, 16 * len(pieces), T.aw[k0:k1, :], T.pb[k0:k1, i * TK:(i + 1) * TK]))
+    mms.append((S.z, 32 if FL else 16, T.aw[:], T.zu[:]))
+    if FL:
+        mms.append((None, 0, T.aw[:], T.zv[:]))
+    for i, (sem, val, lhsT, rhs) in enumerate(mms):
+        if sem is not None:
+            g.tensor.wait_ge(sem, val)
+        last = i == len(mms) - 1
+        ins = g.tensor.matmul(T.acc[:], lhsT, rhs, i == 0, last)
+        if last:
+            ins.then_inc(S.mm, 1)
+
+    g.vector.wait_ge(S.mm, 1)
+    g.vector.tensor_copy(T.ys[:], T.acc[:]).then_inc(S.cp, 1)
+    g.sync.wait_ge(S.cp, 1)
+    g.sync.dma_start(T.y[:], T.ys[:]).then_inc(S.st, 16)
+    g.sync.wait_ge(S.st, 16)
+
+    g.wait_ge(S.loc1, n_loc1)
+    if not FF:
+        g.wait_ge(S.loc2, E2)
+    g.wait_ge(S.loc3, n_loc3)
+    if not FL:
+        g.wait_ge(S.loc4, E4)

@@ -1,24 +1,27 @@
 from concourse.bass import DstId, RemoteDMATransfer
 
 P, TK, NB = 128, 512, 4
-FF = False
-FL = False
-E1, EF, E2, E3, E4 = 2, 2, 8, 8, 8
+W = TK // NB
+E1, E2, E4 = 4, 8, 16
 
 SCRATCH = {
-    "xd": ("dram", [NB, P, P], "bfloat16"),
-    "L": ("dram", [2 * NB if FF else NB, P, P], "bfloat16"),
-    "su": ("dram", [NB, P, P], "bfloat16"),
-    "sv": ("dram", [NB if FL else 1, P, P], "bfloat16"),
+    "xd": ("dram", [NB, P, W], "bfloat16"),
+    "L": ("dram", [NB, P, W], "bfloat16"),
+    "ub": ("dram", [P, W], "bfloat16"),
+    "rv": ("dram", [P, W], "bfloat16"),
     "xs": ("sbuf", [P, TK], "bfloat16"),
     "aw": ("sbuf", [P, P], "bfloat16"),
-    "pb": ("sbuf", [P, (2 * NB if FF else NB) * TK], "bfloat16"),
-    "zu": ("sbuf", [P, TK], "bfloat16"),
-    "zv": ("sbuf", [P, TK if FL else 8], "bfloat16"),
+    "pu": ("sbuf", [P, W], "bfloat16"),
+    "pr": ("sbuf", [P, W], "bfloat16"),
+    "zs": ("sbuf", [P, TK], "bfloat16"),
     "ys": ("sbuf", [P, TK], "bfloat16"),
-    "acc": ("psum", [P, TK], "float32"),
+    "acc0": ("psum", [P, 512], "float32"),
+    "acc1": ("psum", [P, 512], "float32"),
+    "acc2": ("psum", [P, 512], "float32"),
+    "acc3": ("psum", [P, 512], "float32"),
 }
-SEMAPHORES = ["ld", "pre", "pc", "z", "mm", "cp", "st", "l1", "ra", "rb", "ag", "loc1", "loc2", "loc3", "loc4"]
+SEMAPHORES = ["ld", "ow", "pre", "pc", "pd", "mm0", "mm1", "mm2", "mm3", "cp", "st",
+              "l1", "ra", "rb", "ua", "ag", "loc"]
 
 
 def _bits(mask):
@@ -56,22 +59,17 @@ def rank_program(g, core, T, topo):
     assert len(mine) == NB
     q = mine.index(core)
     peers = [c for c in mine if c != core]
-    others = [p for p in chips if p != here]
-    sw = [p for p in others if topo.same_plane(core, members[p][q])][0]
-    cb = [p for p in others if topo.rack(p[0]) != topo.rack(here[0]) and topo.may_write(core, members[p][q])][0]
+    twins = [members[p][q] for p in chips if p != here]
+    sw = [c for c in twins if topo.same_plane(core, c)][0]
+    cb = [c for c in twins if topo.rack(topo.host(c)) != topo.rack(here[0]) and topo.may_write(core, c)][0]
+    near, far = (sw, cb) if q % 2 == 0 else (cb, sw)
 
-    def near(b):
-        return sw if b % 2 == 0 else cb
-
-    def far(b):
-        return cb if b % 2 == 0 else sw
-
-    off = topo.mask(core, members[sw][q]) & topo.mask(core, members[cb][q])
-    onc = off | 0
+    off = topo.mask(core, sw) & topo.mask(core, cb)
+    onc = off
     for c in peers:
         onc |= topo.mask(core, c)
     lo = _bits(off)
-    hi = _bits(onc & ~off)
+    every = lo + _bits(onc & ~off)
 
     def to(c):
         rid, pid = topo.addr(c, core)
@@ -84,99 +82,61 @@ def rank_program(g, core, T, topo):
         return RemoteDMATransfer(dst_ids=[to(c) for c in cs], dma_engine_mask=_mask(engines), remote_sem=sem,
                                  srcs=srcs, dsts=[dst for c in cs], alu_op=1)
 
-    k0, k1 = q * (P // NB), (q + 1) * (P // NB)
+    def blk(t, b):
+        return t[:, b * W:(b + 1) * W]
 
-    g.sync.dma_start(T.xd[:], T.x[:]).then_inc(S.ld, 16)
-    g.scalar.wait_ge(S.ld, 16)
+    queues = [g.sync, g.scalar]
+    rest = [b for b in range(NB) if b != q]
+
+    for i, b in enumerate(rest):
+        queues[i % 2].dma_start(T.xd[b], blk(T.x, b)).then_inc(S.ld, 16)
+    n_ld = 16 * len(rest)
+    g.scalar.dma_start(T.xd[q], blk(T.x, q)).then_inc(S.ow, 16)
+    g.scalar.wait_ge(S.ld, n_ld)
     g.scalar.dma_start(T.xs[:], T.x[:]).then_inc(S.pre, 16)
     g.scalar.dma_start(T.aw[:], T.a[:]).then_inc(S.pre, 16)
 
-    on1 = hi if FF else lo
-    tr = [copy(c, T.xd[mine.index(c)], T.L[q], on1[E1 * i:E1 * (i + 1)], S.l1) for i, c in enumerate(peers)]
+    g.wait_ge(S.ld, n_ld)
+    g.remote_dma_fused([copy(c, T.xd[mine.index(c)], T.L[q], every[E1 * i:E1 * (i + 1)], S.l1)
+                        for i, c in enumerate(peers)], local_sem=S.loc)
     n_l1 = E1 * len(peers)
-    if FF:
-        for b in range(NB):
-            dst = T.su[b] if (FL and b == q) else T.L[NB + q]
-            tr.append(copy(members[near(b)][b], T.xd[b], dst, lo[EF * b:EF * (b + 1)], S.l1))
-        n_l1 += EF * NB
-    g.wait_ge(S.ld, 16)
-    g.remote_dma_fused(tr, local_sem=S.loc1)
-    n_loc1 = n_l1
-
     g.wait_ge(S.l1, n_l1)
-    srcs = [T.xd[q]] + [T.L[b] for b in range(NB) if b != q]
-    pieces = [b for b in range(NB) if b != q]
-    if FF:
-        for s in range(NB):
-            if FL and s == q:
-                srcs.append(T.su[q])
-            else:
-                srcs.append(T.L[NB + s])
-                pieces.append(NB + s)
-    else:
-        spot = T.su[q] if FL else T.L[q]
-        g.remote_dma_fused([fold([members[near(q)][q]], srcs, spot, lo[:E2], S.ra)], local_sem=S.loc2)
-        g.wait_ge(S.ra, E2)
-        srcs = srcs + [spot]
-        if not FL:
-            pieces.append(q)
-
-    if FL:
-        g.remote_dma_fused([fold(members[far(q)], srcs, T.sv[q], lo[:E3], S.rb),
-                            fold(peers, srcs, T.su[q], hi[:E4], S.ag)], local_sem=S.loc3)
-        n_rb, n_loc3 = E3 * NB, E3 + E4
-    else:
-        g.remote_dma_fused([fold([members[far(q)][q]], srcs, T.su[q], lo[:E3], S.rb)], local_sem=S.loc3)
-        n_rb, n_loc3 = E3, E3
-        g.wait_ge(S.rb, n_rb)
-        g.remote_dma_fused([fold(peers, srcs + [T.su[q]], T.su[q], lo[:E4], S.ag)], local_sem=S.loc4)
+    g.wait_ge(S.ow, 16)
+    srcs = [T.xd[q]] + [T.L[b] for b in rest]
+    g.remote_dma_fused([fold([near], srcs, T.L[q], lo[:E2], S.ra)], local_sem=S.loc)
+    g.wait_ge(S.ra, E2)
+    srcs = srcs + [T.L[q]]
+    g.remote_dma_fused([fold([far], srcs, T.rv[:], lo[:E2], S.rb)], local_sem=S.loc)
+    g.remote_dma_fused([fold([near], srcs, T.ub[:], lo[:E2], S.ua)], local_sem=S.loc)
+    g.wait_ge(S.rb, E2)
+    g.remote_dma_fused([fold(peers, srcs + [T.rv[:]], blk(T.zs, q), every[:E4], S.ag)], local_sem=S.loc)
     n_ag = E4 * len(peers)
+    n_loc = n_l1 + 3 * E2 + E4
 
-    queues = [g.sync, g.scalar]
-    for Q in queues:
-        Q.wait_ge(S.l1, n_l1)
-        if not FF:
-            Q.wait_ge(S.ra, E2)
-        if not FL:
-            Q.wait_ge(S.loc3, n_loc3)
-        elif not FF:
-            Q.wait_ge(S.loc2, E2)
-    for i, s in enumerate(pieces):
-        queues[i % 2].dma_start(T.pb[k0:k1, i * TK:(i + 1) * TK], T.L[s]).then_inc(S.pc, 16)
+    g.sync.wait_ge(S.rb, E2)
+    g.sync.dma_start(T.pr[:], T.rv[:]).then_inc(S.pd, 16)
+    g.scalar.wait_ge(S.ua, E2)
+    g.scalar.dma_start(T.pu[:], T.ub[:]).then_inc(S.pc, 16)
 
-    g.sync.wait_ge(S.ag, n_ag)
-    if FL:
-        g.scalar.wait_ge(S.rb, n_rb)
-        g.scalar.dma_start(T.zv[:], T.sv[:]).then_inc(S.z, 16)
-    else:
-        g.sync.wait_ge(S.rb, n_rb)
-    g.sync.dma_start(T.zu[:], T.su[:]).then_inc(S.z, 16)
+    acc = [T["acc%d" % b][:, 0:W] for b in range(NB)]
+    done = [S["mm%d" % b] for b in range(NB)]
+    g.tensor.wait_ge(S.pre, 32)
+    for b in range(NB):
+        for e in range(extra):
+            g.tensor.matmul(acc[b], T.aw[:], blk(T.xs, b), e == 0, False)
+    g.tensor.wait_ge(S.pd, 16)
+    g.tensor.matmul(acc[q], T.aw[:], T.pr[:], extra == 0, False)
+    g.tensor.wait_ge(S.pc, 16)
+    g.tensor.matmul(acc[q], T.aw[:], T.pu[:], False, True).then_inc(done[q], 1)
+    g.tensor.wait_ge(S.ag, n_ag)
+    for b in rest:
+        g.tensor.matmul(acc[b], T.aw[:], blk(T.zs, b), extra == 0, True).then_inc(done[b], 1)
 
-    mms = [(None, 0, T.aw[:], T.xs[:]) for _ in range(extra)]
-    mms.append((None, 0, T.aw[k0:k1, :], T.xs[k0:k1, :]))
-    mms[0] = (S.pre, 32) + mms[0][2:]
-    for i in range(len(pieces)):
-        mms.append((S.pc if i == 0 else None, 16 * len(pieces), T.aw[k0:k1, :], T.pb[k0:k1, i * TK:(i + 1) * TK]))
-    mms.append((S.z, 32 if FL else 16, T.aw[:], T.zu[:]))
-    if FL:
-        mms.append((None, 0, T.aw[:], T.zv[:]))
-    for i, (sem, val, lhsT, rhs) in enumerate(mms):
-        if sem is not None:
-            g.tensor.wait_ge(sem, val)
-        last = i == len(mms) - 1
-        ins = g.tensor.matmul(T.acc[:], lhsT, rhs, i == 0, last)
-        if last:
-            ins.then_inc(S.mm, 1)
-
-    g.vector.wait_ge(S.mm, 1)
-    g.vector.tensor_copy(T.ys[:], T.acc[:]).then_inc(S.cp, 1)
-    g.sync.wait_ge(S.cp, 1)
+    for b in [q] + rest:
+        g.vector.wait_ge(done[b], 1)
+        g.vector.tensor_copy(blk(T.ys, b), acc[b]).then_inc(S.cp, 1)
+    g.sync.wait_ge(S.cp, NB)
     g.sync.dma_start(T.y[:], T.ys[:]).then_inc(S.st, 16)
     g.sync.wait_ge(S.st, 16)
 
-    g.wait_ge(S.loc1, n_loc1)
-    if not FF:
-        g.wait_ge(S.loc2, E2)
-    g.wait_ge(S.loc3, n_loc3)
-    if not FL:
-        g.wait_ge(S.loc4, E4)
+    g.wait_ge(S.loc, n_loc)

@@ -1,12 +1,13 @@
 from concourse.bass import DstId, RemoteDMATransfer
 
-P, TK, NB = 128, 512, 4
-W = TK // NB
+P, TK, NM, NS = 128, 512, 4, 8
+W = TK // NS
 E1, E2, E4 = 4, 8, 16
 
 SCRATCH = {
-    "xd": ("dram", [NB, P, W], "bfloat16"),
-    "L": ("dram", [NB, P, W], "bfloat16"),
+    "xd": ("dram", [NS, P, W], "bfloat16"),
+    "L": ("dram", [NM, P, W], "bfloat16"),
+    "na": ("dram", [P, W], "bfloat16"),
     "ub": ("dram", [P, W], "bfloat16"),
     "rv": ("dram", [P, W], "bfloat16"),
     "xs": ("sbuf", [P, TK], "bfloat16"),
@@ -19,9 +20,11 @@ SCRATCH = {
     "acc1": ("psum", [P, 512], "float32"),
     "acc2": ("psum", [P, 512], "float32"),
     "acc3": ("psum", [P, 512], "float32"),
+    "acc4": ("psum", [P, 512], "float32"),
+    "acc5": ("psum", [P, 512], "float32"),
 }
-SEMAPHORES = ["ld", "ow", "pre", "pc", "pd", "mm0", "mm1", "mm2", "mm3", "cp", "st",
-              "l1", "ra", "rb", "ua", "ag", "loc"]
+SEMAPHORES = ["ldh", "ldm", "ow", "pre", "pc", "pd", "mm0", "mm1", "mm2", "mm3", "mm4", "mm5", "cpm", "cph",
+              "stm", "sth", "l1", "ra", "rb", "ua", "agm", "agh", "loc"]
 
 
 def _bits(mask):
@@ -36,15 +39,10 @@ def _mask(engines):
 
 
 def rank_program(g, core, T, topo):
-    rank = T.rank_of(core)
-    if rank is None:
-        return
     S = T.sem
     coef = T.tables["COEF"]
     n = len(T.cores)
     assert all(coef[r][j] == 1 for r in range(n) for j in range(n) if j != r)
-    extra = coef[rank][rank] - 1
-    assert extra >= 0
 
     def place(c):
         return (topo.host(c), topo.chip(c))
@@ -53,21 +51,35 @@ def rank_program(g, core, T, topo):
     for c in T.cores:
         if place(c) not in chips:
             chips.append(place(c))
-    members = {p: [c for c in T.cores if place(c) == p] for p in chips}
     here = place(core)
+    if here not in chips:
+        return
+    members = {p: [c for c in T.cores if place(c) == p] for p in chips}
+    span = topo.CORES_PER_CHIP
+    owners = {}
+    for p in chips:
+        m = members[p]
+        around = range(max(min(m) - span, 0), max(m) + span)
+        helpers = [c for c in around if place(c) == p and c not in m and topo.die(c) != topo.die(m[0])][:NM]
+        assert len(m) == NM and len(helpers) == NM
+        owners[p] = helpers + m
+    if core not in owners[here]:
+        return
     mine = members[here]
-    assert len(mine) == NB
-    q = mine.index(core)
+    own = owners[here].index(core)
+    member = core in mine
+    q = mine.index(core) if member else None
     peers = [c for c in mine if c != core]
-    twins = [members[p][q] for p in chips if p != here]
+    twins = [owners[p][own] for p in chips if p != here]
     sw = [c for c in twins if topo.same_plane(core, c)][0]
     cb = [c for c in twins if topo.rack(topo.host(c)) != topo.rack(here[0]) and topo.may_write(core, c)][0]
-    near, far = (sw, cb) if q % 2 == 0 else (cb, sw)
+    near, far = (sw, cb) if own % 2 == 0 else (cb, sw)
 
     off = topo.mask(core, sw) & topo.mask(core, cb)
     onc = off
-    for c in peers:
-        onc |= topo.mask(core, c)
+    for c in owners[here]:
+        if c != core:
+            onc |= topo.mask(core, c)
     lo = _bits(off)
     every = lo + _bits(onc & ~off)
 
@@ -85,58 +97,85 @@ def rank_program(g, core, T, topo):
     def blk(t, b):
         return t[:, b * W:(b + 1) * W]
 
-    queues = [g.sync, g.scalar]
-    rest = [b for b in range(NB) if b != q]
+    n_loc = 0
+    if member:
+        queues = [g.sync, g.scalar]
+        for b in range(NM):
+            queues[b % 2].dma_start(T.xd[b], blk(T.x, b)).then_inc(S.ldh, 16)
+        rest = [NM + j for j in range(NM) if j != q]
+        for i, b in enumerate(rest):
+            queues[i % 2].dma_start(T.xd[b], blk(T.x, b)).then_inc(S.ldm, 16)
+        g.scalar.dma_start(T.xd[own], blk(T.x, own)).then_inc(S.ow, 16)
+        g.scalar.wait_ge(S.ldm, 16 * len(rest))
+        g.scalar.dma_start(T.xs[:], T.x[:]).then_inc(S.pre, 16)
+        g.scalar.dma_start(T.aw[:], T.a[:]).then_inc(S.pre, 16)
 
-    for i, b in enumerate(rest):
-        queues[i % 2].dma_start(T.xd[b], blk(T.x, b)).then_inc(S.ld, 16)
-    n_ld = 16 * len(rest)
-    g.scalar.dma_start(T.xd[q], blk(T.x, q)).then_inc(S.ow, 16)
-    g.scalar.wait_ge(S.ld, n_ld)
-    g.scalar.dma_start(T.xs[:], T.x[:]).then_inc(S.pre, 16)
-    g.scalar.dma_start(T.aw[:], T.a[:]).then_inc(S.pre, 16)
+        g.wait_ge(S.ldh, 16 * NM)
+        g.remote_dma_fused([copy(owners[here][b], T.xd[b], T.L[q], every[E1 * b:E1 * (b + 1)], S.l1)
+                            for b in range(NM)], local_sem=S.loc)
+        g.wait_ge(S.ldm, 16 * len(rest))
+        g.remote_dma_fused([copy(owners[here][b], T.xd[b], T.L[q], every[E1 * i:E1 * (i + 1)], S.l1)
+                            for i, b in enumerate(rest)], local_sem=S.loc)
+        n_loc += E1 * (NM + len(rest))
+        srcs = [T.xd[own]] + [T.L[j] for j in range(NM) if j != q]
+        g.wait_ge(S.ow, 16)
+    else:
+        srcs = [T.L[j] for j in range(NM)]
 
-    g.wait_ge(S.ld, n_ld)
-    g.remote_dma_fused([copy(c, T.xd[mine.index(c)], T.L[q], every[E1 * i:E1 * (i + 1)], S.l1)
-                        for i, c in enumerate(peers)], local_sem=S.loc)
-    n_l1 = E1 * len(peers)
-    g.wait_ge(S.l1, n_l1)
-    g.wait_ge(S.ow, 16)
-    srcs = [T.xd[q]] + [T.L[b] for b in rest]
-    g.remote_dma_fused([fold([near], srcs, T.L[q], lo[:E2], S.ra)], local_sem=S.loc)
+    g.wait_ge(S.l1, E1 * len(peers))
+    g.remote_dma_fused([fold([near], srcs, T.na[:], lo[:E2], S.ra)], local_sem=S.loc)
     g.wait_ge(S.ra, E2)
-    srcs = srcs + [T.L[q]]
+    srcs = srcs + [T.na[:]]
     g.remote_dma_fused([fold([far], srcs, T.rv[:], lo[:E2], S.rb)], local_sem=S.loc)
-    g.remote_dma_fused([fold([near], srcs, T.ub[:], lo[:E2], S.ua)], local_sem=S.loc)
+    n_loc += 2 * E2
+    if member:
+        g.remote_dma_fused([fold([near], srcs, T.ub[:], lo[:E2], S.ua)], local_sem=S.loc)
+        n_loc += E2
     g.wait_ge(S.rb, E2)
-    g.remote_dma_fused([fold(peers, srcs + [T.rv[:]], blk(T.zs, q), every[:E4], S.ag)], local_sem=S.loc)
-    n_ag = E4 * len(peers)
-    n_loc = n_l1 + 3 * E2 + E4
+    g.remote_dma_fused([fold(peers, srcs + [T.rv[:]], blk(T.zs, own), every[:E4], S.agm if member else S.agh)],
+                       local_sem=S.loc)
+    n_loc += E4
 
-    g.sync.wait_ge(S.rb, E2)
-    g.sync.dma_start(T.pr[:], T.rv[:]).then_inc(S.pd, 16)
-    g.scalar.wait_ge(S.ua, E2)
-    g.scalar.dma_start(T.pu[:], T.ub[:]).then_inc(S.pc, 16)
+    if member:
+        extra = coef[T.rank_of(core)][T.rank_of(core)] - 1
+        assert extra >= 0
+        g.sync.wait_ge(S.rb, E2)
+        g.sync.dma_start(T.pr[:], T.rv[:]).then_inc(S.pd, 16)
+        g.scalar.wait_ge(S.ua, E2)
+        g.scalar.dma_start(T.pu[:], T.ub[:]).then_inc(S.pc, 16)
 
-    acc = [T["acc%d" % b][:, 0:W] for b in range(NB)]
-    done = [S["mm%d" % b] for b in range(NB)]
-    g.tensor.wait_ge(S.pre, 32)
-    for b in range(NB):
-        for e in range(extra):
-            g.tensor.matmul(acc[b], T.aw[:], blk(T.xs, b), e == 0, False)
-    g.tensor.wait_ge(S.pd, 16)
-    g.tensor.matmul(acc[q], T.aw[:], T.pr[:], extra == 0, False)
-    g.tensor.wait_ge(S.pc, 16)
-    g.tensor.matmul(acc[q], T.aw[:], T.pu[:], False, True).then_inc(done[q], 1)
-    g.tensor.wait_ge(S.ag, n_ag)
-    for b in rest:
-        g.tensor.matmul(acc[b], T.aw[:], blk(T.zs, b), extra == 0, True).then_inc(done[b], 1)
+        half = NM * W
+        cols = [(0, half // 2), (half // 2, half)] + [((NM + j) * W, (NM + j + 1) * W) for j in range(NM)]
+        acc = [T["acc%d" % i][:, 0:c1 - c0] for i, (c0, c1) in enumerate(cols)]
+        done = [S["mm%d" % i] for i in range(len(cols))]
+        mo = 2 + q
+        others = [2 + j for j in range(NM) if j != q]
+        g.tensor.wait_ge(S.pre, 32)
+        for i, (c0, c1) in enumerate(cols):
+            for e in range(extra):
+                g.tensor.matmul(acc[i], T.aw[:], T.xs[:, c0:c1], e == 0, False)
+        g.tensor.wait_ge(S.pd, 16)
+        g.tensor.matmul(acc[mo], T.aw[:], T.pr[:], extra == 0, False)
+        g.tensor.wait_ge(S.pc, 16)
+        g.tensor.matmul(acc[mo], T.aw[:], T.pu[:], False, True).then_inc(done[mo], 1)
+        g.tensor.wait_ge(S.agm, E4 * len(peers))
+        for i in others:
+            g.tensor.matmul(acc[i], T.aw[:], T.zs[:, cols[i][0]:cols[i][1]], extra == 0, True).then_inc(done[i], 1)
+        g.tensor.wait_ge(S.agh, E4 * NM)
+        for i in (0, 1):
+            g.tensor.matmul(acc[i], T.aw[:], T.zs[:, cols[i][0]:cols[i][1]], extra == 0, True).then_inc(done[i], 1)
 
-    for b in [q] + rest:
-        g.vector.wait_ge(done[b], 1)
-        g.vector.tensor_copy(blk(T.ys, b), acc[b]).then_inc(S.cp, 1)
-    g.sync.wait_ge(S.cp, NB)
-    g.sync.dma_start(T.y[:], T.ys[:]).then_inc(S.st, 16)
-    g.sync.wait_ge(S.st, 16)
+        for i in [mo] + others:
+            g.vector.wait_ge(done[i], 1)
+            g.vector.tensor_copy(T.ys[:, cols[i][0]:cols[i][1]], acc[i]).then_inc(S.cpm, 1)
+        for i in (0, 1):
+            g.vector.wait_ge(done[i], 1)
+            g.vector.tensor_copy(T.ys[:, cols[i][0]:cols[i][1]], acc[i]).then_inc(S.cph, 1)
+        g.scalar.wait_ge(S.cpm, NM)
+        g.scalar.dma_start(T.y[:, half:TK], T.ys[:, half:TK]).then_inc(S.stm, 16)
+        g.scalar.wait_ge(S.stm, 16)
+        g.sync.wait_ge(S.cph, 2)
+        g.sync.dma_start(T.y[:, 0:half], T.ys[:, 0:half]).then_inc(S.sth, 16)
+        g.sync.wait_ge(S.sth, 16)
 
     g.wait_ge(S.loc, n_loc)

@@ -1,19 +1,25 @@
 from concourse.bass import DstId, RemoteDMATransfer
 
-P, TK, NM, NS = 128, 512, 4, 8
-W = TK // NS
-E1, E2, E4 = 4, 8, 16
+P, TK, NM = 128, 512, 4
+WH = 48
+WM = TK // NM - WH
+E1, E2, E4, EA = 4, 8, 16, 2
 
 SCRATCH = {
-    "xd": ("dram", [NS, P, W], "bfloat16"),
-    "L": ("dram", [NM, P, W], "bfloat16"),
-    "na": ("dram", [P, W], "bfloat16"),
-    "ub": ("dram", [P, W], "bfloat16"),
-    "rv": ("dram", [P, W], "bfloat16"),
+    "xdh": ("dram", [NM, P, WH], "bfloat16"),
+    "xdm": ("dram", [NM, P, WM], "bfloat16"),
+    "Lh": ("dram", [NM, P, WH], "bfloat16"),
+    "Lm": ("dram", [NM, P, WM], "bfloat16"),
+    "nah": ("dram", [P, WH], "bfloat16"),
+    "nam": ("dram", [P, WM], "bfloat16"),
+    "rvh": ("dram", [P, WH], "bfloat16"),
+    "rvm": ("dram", [P, WM], "bfloat16"),
+    "La": ("dram", [NM, P, WM], "bfloat16"),
     "xs": ("sbuf", [P, TK], "bfloat16"),
     "aw": ("sbuf", [P, P], "bfloat16"),
-    "pu": ("sbuf", [P, W], "bfloat16"),
-    "pr": ("sbuf", [P, W], "bfloat16"),
+    "pcs": ("sbuf", [P, WM], "bfloat16"),
+    "pn": ("sbuf", [P, WM], "bfloat16"),
+    "pr": ("sbuf", [P, WM], "bfloat16"),
     "zs": ("sbuf", [P, TK], "bfloat16"),
     "ys": ("sbuf", [P, TK], "bfloat16"),
     "acc0": ("psum", [P, 512], "float32"),
@@ -24,7 +30,7 @@ SCRATCH = {
     "acc5": ("psum", [P, 512], "float32"),
 }
 SEMAPHORES = ["ldh", "ldm", "ow", "pre", "pc", "pd", "mm0", "mm1", "mm2", "mm3", "mm4", "mm5", "cpm", "cph",
-              "stm", "sth", "l1", "ra", "rb", "ua", "agm", "agh", "loc"]
+              "stm", "sth", "l1", "ra", "rb", "la", "ca", "s3", "agm", "agh", "loc"]
 
 
 def _bits(mask):
@@ -56,32 +62,32 @@ def rank_program(g, core, T, topo):
         return
     members = {p: [c for c in T.cores if place(c) == p] for p in chips}
     span = topo.CORES_PER_CHIP
-    owners = {}
+    helpers = {}
     for p in chips:
         m = members[p]
         around = range(max(min(m) - span, 0), max(m) + span)
-        helpers = [c for c in around if place(c) == p and c not in m and topo.die(c) != topo.die(m[0])][:NM]
-        assert len(m) == NM and len(helpers) == NM
-        owners[p] = helpers + m
-    if core not in owners[here]:
+        helpers[p] = [c for c in around if place(c) == p and c not in m and topo.die(c) != topo.die(m[0])][:NM]
+        assert len(m) == NM and len(helpers[p]) == NM
+    mine, aides = members[here], helpers[here]
+    if core not in mine + aides:
         return
-    mine = members[here]
-    own = owners[here].index(core)
     member = core in mine
-    q = mine.index(core) if member else None
+    kind = members if member else helpers
+    q = kind[here].index(core)
     peers = [c for c in mine if c != core]
-    twins = [owners[p][own] for p in chips if p != here]
+    twins = [kind[p][q] for p in chips if p != here]
     sw = [c for c in twins if topo.same_plane(core, c)][0]
     cb = [c for c in twins if topo.rack(topo.host(c)) != topo.rack(here[0]) and topo.may_write(core, c)][0]
-    near, far = (sw, cb) if own % 2 == 0 else (cb, sw)
+    near, far = (sw, cb) if q % 2 == 0 else (cb, sw)
 
     off = topo.mask(core, sw) & topo.mask(core, cb)
     onc = off
-    for c in owners[here]:
+    for c in mine + aides:
         if c != core:
             onc |= topo.mask(core, c)
     lo = _bits(off)
-    every = lo + _bits(onc & ~off)
+    hi = _bits(onc & ~off)
+    every = lo + hi
 
     def to(c):
         rid, pid = topo.addr(c, core)
@@ -94,70 +100,84 @@ def rank_program(g, core, T, topo):
         return RemoteDMATransfer(dst_ids=[to(c) for c in cs], dma_engine_mask=_mask(engines), remote_sem=sem,
                                  srcs=srcs, dsts=[dst for c in cs], alu_op=1)
 
-    def blk(t, b):
-        return t[:, b * W:(b + 1) * W]
+    half = NM * WH
+
+    def hcol(t, b):
+        return t[:, b * WH:(b + 1) * WH]
+
+    def mcol(t, j):
+        return t[:, half + j * WM:half + (j + 1) * WM]
 
     n_loc = 0
     if member:
         queues = [g.sync, g.scalar]
+        rest = [j for j in range(NM) if j != q]
         for b in range(NM):
-            queues[b % 2].dma_start(T.xd[b], blk(T.x, b)).then_inc(S.ldh, 16)
-        rest = [NM + j for j in range(NM) if j != q]
-        for i, b in enumerate(rest):
-            queues[i % 2].dma_start(T.xd[b], blk(T.x, b)).then_inc(S.ldm, 16)
-        g.scalar.dma_start(T.xd[own], blk(T.x, own)).then_inc(S.ow, 16)
+            queues[b % 2].dma_start(T.xdh[b], hcol(T.x, b)).then_inc(S.ldh, 16)
+        for i, j in enumerate(rest):
+            queues[i % 2].dma_start(T.xdm[j], mcol(T.x, j)).then_inc(S.ldm, 16)
+        g.scalar.dma_start(T.xdm[q], mcol(T.x, q)).then_inc(S.ow, 16)
         g.scalar.wait_ge(S.ldm, 16 * len(rest))
         g.scalar.dma_start(T.xs[:], T.x[:]).then_inc(S.pre, 16)
         g.scalar.dma_start(T.aw[:], T.a[:]).then_inc(S.pre, 16)
 
         g.wait_ge(S.ldh, 16 * NM)
-        g.remote_dma_fused([copy(owners[here][b], T.xd[b], T.L[q], every[E1 * b:E1 * (b + 1)], S.l1)
+        g.remote_dma_fused([copy(aides[b], T.xdh[b], T.Lh[q], every[E1 * b:E1 * (b + 1)], S.l1)
                             for b in range(NM)], local_sem=S.loc)
         g.wait_ge(S.ldm, 16 * len(rest))
-        g.remote_dma_fused([copy(owners[here][b], T.xd[b], T.L[q], every[E1 * i:E1 * (i + 1)], S.l1)
-                            for i, b in enumerate(rest)], local_sem=S.loc)
+        g.remote_dma_fused([copy(mine[j], T.xdm[j], T.Lm[q], every[E1 * i:E1 * (i + 1)], S.l1)
+                            for i, j in enumerate(rest)], local_sem=S.loc)
         n_loc += E1 * (NM + len(rest))
-        srcs = [T.xd[own]] + [T.L[j] for j in range(NM) if j != q]
+        srcs = [T.xdm[q]] + [T.Lm[j] for j in rest]
+        na, rv, out, ag = T.nam, T.rvm, mcol(T.zs, q), S.agm
         g.wait_ge(S.ow, 16)
     else:
-        srcs = [T.L[j] for j in range(NM)]
+        srcs = [T.Lh[j] for j in range(NM)]
+        na, rv, out, ag = T.nah, T.rvh, hcol(T.zs, q), S.agh
 
     g.wait_ge(S.l1, E1 * len(peers))
-    g.remote_dma_fused([fold([near], srcs, T.na[:], lo[:E2], S.ra)], local_sem=S.loc)
-    g.wait_ge(S.ra, E2)
-    srcs = srcs + [T.na[:]]
-    g.remote_dma_fused([fold([far], srcs, T.rv[:], lo[:E2], S.rb)], local_sem=S.loc)
-    n_loc += 2 * E2
+    g.remote_dma_fused([fold([near], srcs, na[:], lo[:E2], S.ra)], local_sem=S.loc)
+    n_loc += E2
     if member:
-        g.remote_dma_fused([fold([near], srcs, T.ub[:], lo[:E2], S.ua)], local_sem=S.loc)
+        g.remote_dma_fused([copy(aides[j], T.xdm[j], T.La[q], hi[EA * j:EA * (j + 1)], S.la)
+                            for j in range(NM)], local_sem=S.loc)
+        n_loc += EA * NM
+    g.wait_ge(S.ra, E2)
+    srcs = srcs + [na[:]]
+    g.remote_dma_fused([fold([far], srcs, rv[:], lo[:E2], S.rb)], local_sem=S.s3)
+    if not member:
+        g.wait_ge(S.la, EA * NM)
+        g.remote_dma_fused([fold([mine[q]], [T.La[j] for j in range(NM)], T.pcs[:], hi[:E2], S.ca)], local_sem=S.loc)
         n_loc += E2
+        g.wait_ge(S.s3, E2)
     g.wait_ge(S.rb, E2)
-    g.remote_dma_fused([fold(peers, srcs + [T.rv[:]], blk(T.zs, own), every[:E4], S.agm if member else S.agh)],
-                       local_sem=S.loc)
+    g.remote_dma_fused([fold(peers, srcs + [rv[:]], out, every[:E4], ag)], local_sem=S.loc)
     n_loc += E4
 
     if member:
         extra = coef[T.rank_of(core)][T.rank_of(core)] - 1
         assert extra >= 0
+        g.sync.wait_ge(S.ra, E2)
+        g.sync.wait_ge(S.s3, E2)
+        g.sync.dma_start(T.pn[:], T.nam[:]).then_inc(S.pc, 16)
         g.sync.wait_ge(S.rb, E2)
-        g.sync.dma_start(T.pr[:], T.rv[:]).then_inc(S.pd, 16)
-        g.scalar.wait_ge(S.ua, E2)
-        g.scalar.dma_start(T.pu[:], T.ub[:]).then_inc(S.pc, 16)
+        g.sync.dma_start(T.pr[:], T.rvm[:]).then_inc(S.pd, 16)
 
-        half = NM * W
-        cols = [(0, half // 2), (half // 2, half)] + [((NM + j) * W, (NM + j + 1) * W) for j in range(NM)]
+        cols = [(0, half // 2), (half // 2, half)] + [(half + j * WM, half + (j + 1) * WM) for j in range(NM)]
         acc = [T["acc%d" % i][:, 0:c1 - c0] for i, (c0, c1) in enumerate(cols)]
         done = [S["mm%d" % i] for i in range(len(cols))]
         mo = 2 + q
-        others = [2 + j for j in range(NM) if j != q]
+        others = [2 + j for j in rest]
         g.tensor.wait_ge(S.pre, 32)
         for i, (c0, c1) in enumerate(cols):
             for e in range(extra):
                 g.tensor.matmul(acc[i], T.aw[:], T.xs[:, c0:c1], e == 0, False)
-        g.tensor.wait_ge(S.pd, 16)
-        g.tensor.matmul(acc[mo], T.aw[:], T.pr[:], extra == 0, False)
+        g.tensor.wait_ge(S.ca, E2)
+        g.tensor.matmul(acc[mo], T.aw[:], T.pcs[:], extra == 0, False)
         g.tensor.wait_ge(S.pc, 16)
-        g.tensor.matmul(acc[mo], T.aw[:], T.pu[:], False, True).then_inc(done[mo], 1)
+        g.tensor.matmul(acc[mo], T.aw[:], T.pn[:], False, False)
+        g.tensor.wait_ge(S.pd, 16)
+        g.tensor.matmul(acc[mo], T.aw[:], T.pr[:], False, True).then_inc(done[mo], 1)
         g.tensor.wait_ge(S.agm, E4 * len(peers))
         for i in others:
             g.tensor.matmul(acc[i], T.aw[:], T.zs[:, cols[i][0]:cols[i][1]], extra == 0, True).then_inc(done[i], 1)

from concourse.bass import DstId, RemoteDMATransfer

P, TK, NM = 128, 512, 4
WH = 48
WM = TK // NM - WH
E1, E2, E4, EA = 4, 8, 16, 2

SCRATCH = {
    "xdh": ("dram", [NM, P, WH], "bfloat16"),
    "xdm": ("dram", [NM, P, WM], "bfloat16"),
    "Lh": ("dram", [NM, P, WH], "bfloat16"),
    "Lm": ("dram", [NM, P, WM], "bfloat16"),
    "nah": ("dram", [P, WH], "bfloat16"),
    "nam": ("dram", [P, WM], "bfloat16"),
    "rvh": ("dram", [P, WH], "bfloat16"),
    "rvm": ("dram", [P, WM], "bfloat16"),
    "La": ("dram", [NM, P, WM], "bfloat16"),
    "xs": ("sbuf", [P, TK], "bfloat16"),
    "aw": ("sbuf", [P, P], "bfloat16"),
    "pcs": ("sbuf", [P, WM], "bfloat16"),
    "pn": ("sbuf", [P, WM], "bfloat16"),
    "pr": ("sbuf", [P, WM], "bfloat16"),
    "zs": ("sbuf", [P, TK], "bfloat16"),
    "ys": ("sbuf", [P, TK], "bfloat16"),
    "acc0": ("psum", [P, 512], "float32"),
    "acc1": ("psum", [P, 512], "float32"),
    "acc2": ("psum", [P, 512], "float32"),
    "acc3": ("psum", [P, 512], "float32"),
    "acc4": ("psum", [P, 512], "float32"),
    "acc5": ("psum", [P, 512], "float32"),
}
SEMAPHORES = ["ldh", "ldm", "ow", "pre", "pc", "pd", "mm0", "mm1", "mm2", "mm3", "mm4", "mm5", "cpm", "cph",
              "stm", "sth", "l1", "ra", "rb", "la", "ca", "s3", "agm", "agh", "loc"]


def _bits(mask):
    return [e for e in range(mask.bit_length()) if (mask >> e) & 1]


def _mask(engines):
    m = 0
    for e in engines:
        m |= 1 << e
    return m


def rank_program(g, core, T, topo):
    S = T.sem
    coef = T.tables["COEF"]
    n = len(T.cores)
    assert all(coef[r][j] == 1 for r in range(n) for j in range(n) if j != r)

    def place(c):
        return (topo.host(c), topo.chip(c))

    chips = []
    for c in T.cores:
        if place(c) not in chips:
            chips.append(place(c))
    here = place(core)
    if here not in chips:
        return
    members = {p: [c for c in T.cores if place(c) == p] for p in chips}
    span = topo.CORES_PER_CHIP
    helpers = {}
    for p in chips:
        m = members[p]
        around = range(max(min(m) - span, 0), max(m) + span)
        helpers[p] = [c for c in around if place(c) == p and c not in m and topo.die(c) != topo.die(m[0])][:NM]
        assert len(m) == NM and len(helpers[p]) == NM
    mine, aides = members[here], helpers[here]
    if core not in mine + aides:
        return
    member = core in mine
    kind = members if member else helpers
    q = kind[here].index(core)
    peers = [c for c in mine if c != core]
    twins = [kind[p][q] for p in chips if p != here]
    sw = [c for c in twins if topo.same_plane(core, c)][0]
    cb = [c for c in twins if topo.rack(topo.host(c)) != topo.rack(here[0]) and topo.may_write(core, c)][0]
    near, far = (sw, cb) if q % 2 == 0 else (cb, sw)

    off = topo.mask(core, sw) & topo.mask(core, cb)
    onc = off
    for c in mine + aides:
        if c != core:
            onc |= topo.mask(core, c)
    lo = _bits(off)
    hi = _bits(onc & ~off)
    every = lo + hi

    def to(c):
        rid, pid = topo.addr(c, core)
        return DstId(rid=rid, pnc=pid)

    def copy(c, src, dst, engines, sem):
        return RemoteDMATransfer(dst_ids=[to(c)], dma_engine_mask=_mask(engines), remote_sem=sem, src=src, dst=dst)

    def fold(cs, srcs, dst, engines, sem):
        return RemoteDMATransfer(dst_ids=[to(c) for c in cs], dma_engine_mask=_mask(engines), remote_sem=sem,
                                 srcs=srcs, dsts=[dst for c in cs], alu_op=1)

    half = NM * WH

    def hcol(t, b):
        return t[:, b * WH:(b + 1) * WH]

    def mcol(t, j):
        return t[:, half + j * WM:half + (j + 1) * WM]

    n_loc = 0
    if member:
        queues = [g.sync, g.scalar]
        rest = [j for j in range(NM) if j != q]
        for b in range(NM):
            queues[b % 2].dma_start(T.xdh[b], hcol(T.x, b)).then_inc(S.ldh, 16)
        for i, j in enumerate(rest):
            queues[i % 2].dma_start(T.xdm[j], mcol(T.x, j)).then_inc(S.ldm, 16)
        g.scalar.dma_start(T.xdm[q], mcol(T.x, q)).then_inc(S.ow, 16)
        g.scalar.wait_ge(S.ldm, 16 * len(rest))
        g.scalar.dma_start(T.xs[:], T.x[:]).then_inc(S.pre, 16)
        g.scalar.dma_start(T.aw[:], T.a[:]).then_inc(S.pre, 16)

        g.wait_ge(S.ldh, 16 * NM)
        g.remote_dma_fused([copy(aides[b], T.xdh[b], T.Lh[q], every[E1 * b:E1 * (b + 1)], S.l1)
                            for b in range(NM)], local_sem=S.loc)
        g.wait_ge(S.ldm, 16 * len(rest))
        g.remote_dma_fused([copy(mine[j], T.xdm[j], T.Lm[q], every[E1 * i:E1 * (i + 1)], S.l1)
                            for i, j in enumerate(rest)], local_sem=S.loc)
        n_loc += E1 * (NM + len(rest))
        srcs = [T.xdm[q]] + [T.Lm[j] for j in rest]
        na, rv, out, ag = T.nam, T.rvm, mcol(T.zs, q), S.agm
        g.wait_ge(S.ow, 16)
    else:
        srcs = [T.Lh[j] for j in range(NM)]
        na, rv, out, ag = T.nah, T.rvh, hcol(T.zs, q), S.agh

    g.wait_ge(S.l1, E1 * len(peers))
    g.remote_dma_fused([fold([near], srcs, na[:], lo[:E2], S.ra)], local_sem=S.loc)
    n_loc += E2
    if member:
        g.remote_dma_fused([copy(aides[j], T.xdm[j], T.La[q], hi[EA * j:EA * (j + 1)], S.la)
                            for j in range(NM)], local_sem=S.loc)
        n_loc += EA * NM
    g.wait_ge(S.ra, E2)
    srcs = srcs + [na[:]]
    g.remote_dma_fused([fold([far], srcs, rv[:], lo[:E2], S.rb)], local_sem=S.s3)
    if not member:
        g.wait_ge(S.la, EA * NM)
        g.remote_dma_fused([fold([mine[q]], [T.La[j] for j in range(NM)], T.pcs[:], hi[:E2], S.ca)], local_sem=S.loc)
        n_loc += E2
        g.wait_ge(S.s3, E2)
    g.wait_ge(S.rb, E2)
    g.remote_dma_fused([fold(peers, srcs + [rv[:]], out, every[:E4], ag)], local_sem=S.loc)
    n_loc += E4

    if member:
        extra = coef[T.rank_of(core)][T.rank_of(core)] - 1
        assert extra >= 0
        g.sync.wait_ge(S.ra, E2)
        g.sync.wait_ge(S.s3, E2)
        g.sync.dma_start(T.pn[:], T.nam[:]).then_inc(S.pc, 16)
        g.sync.wait_ge(S.rb, E2)
        g.sync.dma_start(T.pr[:], T.rvm[:]).then_inc(S.pd, 16)

        cols = [(0, half // 2), (half // 2, half)] + [(half + j * WM, half + (j + 1) * WM) for j in range(NM)]
        acc = [T["acc%d" % i][:, 0:c1 - c0] for i, (c0, c1) in enumerate(cols)]
        done = [S["mm%d" % i] for i in range(len(cols))]
        mo = 2 + q
        others = [2 + j for j in rest]
        g.tensor.wait_ge(S.pre, 32)
        for i, (c0, c1) in enumerate(cols):
            for e in range(extra):
                g.tensor.matmul(acc[i], T.aw[:], T.xs[:, c0:c1], e == 0, False)
        g.tensor.wait_ge(S.ca, E2)
        g.tensor.matmul(acc[mo], T.aw[:], T.pcs[:], extra == 0, False)
        g.tensor.wait_ge(S.pc, 16)
        g.tensor.matmul(acc[mo], T.aw[:], T.pn[:], False, False)
        g.tensor.wait_ge(S.pd, 16)
        g.tensor.matmul(acc[mo], T.aw[:], T.pr[:], False, True).then_inc(done[mo], 1)
        g.tensor.wait_ge(S.agm, E4 * len(peers))
        for i in others:
            g.tensor.matmul(acc[i], T.aw[:], T.zs[:, cols[i][0]:cols[i][1]], extra == 0, True).then_inc(done[i], 1)
        g.tensor.wait_ge(S.agh, E4 * NM)
        for i in (0, 1):
            g.tensor.matmul(acc[i], T.aw[:], T.zs[:, cols[i][0]:cols[i][1]], extra == 0, True).then_inc(done[i], 1)

        for i in [mo] + others:
            g.vector.wait_ge(done[i], 1)
            g.vector.tensor_copy(T.ys[:, cols[i][0]:cols[i][1]], acc[i]).then_inc(S.cpm, 1)
        for i in (0, 1):
            g.vector.wait_ge(done[i], 1)
            g.vector.tensor_copy(T.ys[:, cols[i][0]:cols[i][1]], acc[i]).then_inc(S.cph, 1)
        g.scalar.wait_ge(S.cpm, NM)
        g.scalar.dma_start(T.y[:, half:TK], T.ys[:, half:TK]).then_inc(S.stm, 16)
        g.scalar.wait_ge(S.stm, 16)
        g.sync.wait_ge(S.cph, 2)
        g.sync.dma_start(T.y[:, 0:half], T.ys[:, 0:half]).then_inc(S.sth, 16)
        g.sync.wait_ge(S.sth, 16)

    g.wait_ge(S.loc, n_loc)
